import numpy as np
import ml_dtypes


def mxq(x, axis, fmt="e4m3"):
    dtype, down = {"e4m3": (ml_dtypes.float8_e4m3fn, 7), "e5m2": (ml_dtypes.float8_e5m2, 14)}[fmt]
    v = np.moveaxis(np.asarray(x, np.float32).astype(ml_dtypes.bfloat16).astype(np.float64), axis, -1)
    blocks = v.reshape(v.shape[:-1] + (-1, 32))
    amax = np.abs(blocks).max(-1, keepdims=True)
    byte = np.maximum(np.where(amax > 0, np.frexp(amax)[1] - 1 + 127, 0) - down, 1)
    scale = np.exp2(byte - 127.0)
    codes = (blocks / scale).astype(np.float32).astype(dtype).astype(np.float64)
    return np.moveaxis((codes * scale).reshape(v.shape), -1, axis)


WIDE = False


def mx_kscale(k):
    if not WIDE:
        return np.ones(k)
    levels = np.array([10, -10, 5, -5, 0])
    if k % 512:
        return np.exp2(np.random.permutation(np.resize(levels, k // 32))).repeat(32)
    a = np.empty((k // 512, 16))
    for p in range(k // 512):
        a[p, :8] = np.random.permutation(np.resize(levels, 8))
        for g in range(8):
            far = levels[np.abs(levels - a[p, g]) >= 10]
            a[p, g + 8] = far[np.random.randint(len(far))]
    return np.exp2(a.ravel()).repeat(32)


def f64(x):
    return np.asarray(x).astype(np.float64)


def striped8(idx):
    return np.concatenate([v.reshape(-1, 16).T for v in idx]).astype(np.uint16)


def unstriped8(offs):
    return np.stack([offs[16 * g:16 * g + 16].T.reshape(-1) for g in range(8)]).astype(np.int64)


K, M, T, S = 512, 1024, 1024, 512


def setup_inputs():
    n = np.random.standard_normal
    s = mx_kscale(K)[:, None]
    return {
        "xT": (n((K, T)) * s).astype(np.float32),
        "w": (n((K, M)) / np.sqrt(K) / s).astype(np.float32),
        "wgt": np.repeat(np.random.uniform(0.5, 2.0, (8, S)), 16, axis=0).astype(np.float32),
        "wgo": np.repeat(np.random.uniform(0.5, 2.0, (8, S)), 16, axis=0).astype(np.float32),
        "offs": striped8(np.stack([np.random.permutation(T)[:S] for _ in range(8)])),
        "offs2": striped8(np.stack([np.random.permutation(T)[:S] for _ in range(8)])),
    }


def reference(xT, w, wgt, wgo, offs, offs2):
    idx = unstriped8(offs)
    group = np.arange(K) % 512 // 64
    xg = f64(wgt)[np.arange(K) // 4 % 128] * f64(xT)[np.arange(K)[:, None], idx[group]]
    xT_ = mxq(xg, 0, "e4m3")
    w_ = mxq(f64(w), 0, "e4m3")
    y = w_.T @ xT_
    place = unstriped8(offs2)[np.arange(M) % 128 // 16]
    out = np.zeros((M, T))
    out[np.arange(M)[:, None], place] = f64(wgo)[np.arange(M) % 128] * (y)
    return out

@@ -1,0 +1,160 @@
+import concourse.mybir as mybir
+
+K, M, T, S = 512, 1024, 1024, 512
+FLOPS = 2 * K * M * S
+
+F32 = mybir.dt.float32
+BF16 = mybir.dt.bfloat16
+U32 = mybir.dt.uint32
+U16 = mybir.dt.uint16
+U8 = mybir.dt.uint8
+FP8X4 = mybir.dt.float8_e4m3fn_x4
+MULT = mybir.AluOpType.mult
+
+P = 128
+PACK = 4
+HALF = S // 2
+LIST_COLS = S // 16
+HALF_COLS = LIST_COLS // 2
+BLOCKS = M // P
+
+
+def tile_list_hboth_none_kernel(tc, xT, w, wgt, wgo, offs, offs2, out):
+    nc = tc.nc
+    x_planes = xT.rearrange("(p i) t -> p i t", i=PACK)
+    w_rows = w.rearrange("(p i) n -> p i n", i=PACK)
+
+    with (
+        tc.tile_pool(name="held", bufs=1) as held,
+        tc.psum_pool(name="psum", bufs=1) as psum,
+    ):
+        list_in = held.tile([P, LIST_COLS], U16, name="list_in")
+        list_out = held.tile([P, LIST_COLS], U16, name="list_out")
+        wgt_half = [held.tile([P, HALF], F32, name=f"wgt{h}") for h in range(2)]
+        wgo_all = held.tile([P, S], F32, name="wgo_all")
+        planes = [held.tile([P, T], F32, name=f"plane{i}") for i in range(PACK)]
+        windows = [held.tile([P, T], F32, name=f"window{b}") for b in range(BLOCKS)]
+
+        nc.sync.dma_start(list_in[:], offs)
+        nc.scalar.dma_start(wgt_half[0][:], wgt[:, 0:HALF])
+        nc.sync.dma_start(planes[0][:], x_planes[:, 0, :])
+        nc.scalar.dma_start(wgt_half[1][:], wgt[:, HALF:S])
+        for i in range(1, PACK):
+            nc.sync.dma_start(planes[i][:], x_planes[:, i, :])
+
+        for b in range(BLOCKS):
+            nc.gpsimd.memset(windows[b][:], 0.0)
+
+        w_loads = [(0, 128), (128, 384), (512, 512)]
+        w_raw = []
+        for n, (c0, width) in enumerate(w_loads):
+            raw = held.tile([P, PACK, width], F32, name=f"w_raw{n}")
+            nc.sync.dma_start(raw[:], w_rows[:, :, c0 : c0 + width])
+            w_raw.append(raw)
+            if n == 0:
+                nc.sync.dma_start(list_out[:], offs2)
+                nc.sync.dma_start(wgo_all[:], wgo)
+
+        gathered = [held.tile([P, PACK, HALF], F32, name=f"gathered{h}") for h in range(2)]
+        x_grouped = [held.tile([P, HALF, PACK], BF16, align_bytes=64, name=f"x_grouped{h}") for h in range(2)]
+        x_codes = held.tile([P, S], U32, align_bytes=64, name="x_codes")
+        x_scales = held.tile([P, S], U8, align_bytes=64, name="x_scales")
+
+        def gather(i, h):
+            nc.vector.tensor_tensor(
+                gathered[h][:, i, :],
+                planes[i][:].indirect(list_in[:, h * HALF_COLS : (h + 1) * HALF_COLS]),
+                wgt_half[h][:],
+                MULT,
+            )
+
+        def interleave(copy, grouped, rows):
+            copy(
+                out=grouped.rearrange("p (c i) t -> p c t i", i=4),
+                in_=rows.rearrange("p t (c i) -> p c t i", i=4),
+            )
+
+        def quantize_x(h):
+            cols = slice(h * HALF, (h + 1) * HALF)
+            nc.vector.quantize_mx(
+                out=x_codes[:, cols].bitcast(FP8X4),
+                scales=x_scales[:, cols],
+                in_=x_grouped[h][:].rearrange("p c t -> p (c t)"),
+            )
+
+        w_codes = {}
+
+        def prepare_w(n, c0, width):
+            start = w_loads[n][0]
+            grouped = held.tile([P, width, PACK], BF16, align_bytes=64, name=f"w_grouped{c0}")
+            codes = held.tile([P, width], U32, align_bytes=64, name=f"w_codes{c0}")
+            scales = held.tile([P, width], U8, align_bytes=64, name=f"w_scales{c0}")
+            interleave(nc.scalar.copy, grouped[:], w_raw[n][:, :, c0 - start : c0 - start + width])
+            nc.vector.quantize_mx(
+                out=codes[:].bitcast(FP8X4),
+                scales=scales[:],
+                in_=grouped[:].rearrange("p c t -> p (c t)"),
+            )
+            for b in range(c0 // P, (c0 + width) // P):
+                cols = slice(b * P - c0, (b + 1) * P - c0)
+                w_codes[b] = (codes[:, cols].bitcast(FP8X4), scales[:, cols])
+
+        y = {}
+
+        def product(b, h0, h1):
+            cols = slice(h0 * HALF, h1 * HALF)
+            width = (h1 - h0) * HALF
+            bank = psum.tile([P, width], F32, name=f"bank{b % 4}_{h0}" if b < 2 else f"wide{b % 4}")
+            nc.tensor.matmul_mx(
+                out=bank[:],
+                lhsT=w_codes[b][0],
+                lhsT_scale=w_codes[b][1],
+                rhs=x_codes[:, cols].bitcast(FP8X4),
+                rhs_scale=x_scales[:, cols],
+                start=True,
+                stop=True,
+            )
+            rows = held.tile([P, width], F32, name=f"y{b}_{h0}")
+            nc.scalar.copy(out=rows[:], in_=bank[:])
+            for h in range(h0, h1):
+                y[b, h] = rows[:, (h - h0) * HALF : (h - h0 + 1) * HALF]
+
+        def scatter(b, h):
+            nc.vector.tensor_tensor(
+                windows[b][:].indirect(list_out[:, h * HALF_COLS : (h + 1) * HALF_COLS]),
+                y[b, h],
+                wgo_all[:, h * HALF : (h + 1) * HALF],
+                MULT,
+            )
+
+        def store(b):
+            nc.sync.dma_start(out[b * P : (b + 1) * P, :], windows[b][:])
+
+        for i, h in ((0, 0), (0, 1), (1, 0), (1, 1), (2, 0), (2, 1), (3, 0)):
+            gather(i, h)
+        interleave(nc.vector.tensor_copy, x_grouped[0][:], gathered[0][:])
+        prepare_w(0, 0, 128)
+        quantize_x(0)
+        gather(3, 1)
+        prepare_w(1, 128, 128)
+        product(0, 0, 1)
+        interleave(nc.scalar.copy, x_grouped[1][:], gathered[1][:])
+        product(1, 0, 1)
+        scatter(0, 0)
+        quantize_x(1)
+        scatter(1, 0)
+        product(0, 1, 2)
+        product(1, 1, 2)
+        prepare_w(1, 256, 256)
+        scatter(0, 1)
+        store(0)
+        product(2, 0, 2)
+        prepare_w(2, 512, 512)
+        for b in range(2, BLOCKS):
+            if b + 1 < BLOCKS:
+                product(b + 1, 0, 2)
+            scatter(b, 0)
+            scatter(b - 1, 1)
+            store(b - 1)
+        scatter(BLOCKS - 1, 1)
+        store(BLOCKS - 1)

@@ -42,7 +42,11 @@ def tile_list_hboth_none_kernel(tc, xT, w, wgt, wgo, offs, offs2, out):
         for i in range(1, PACK):
             nc.sync.dma_start(planes[i][:], x_planes[:, i, :])
 
-        for b in range(BLOCKS):
+        for b in range(6):
+            nc.vector.memset(windows[b][:], 0.0)
+        for b in range(6, BLOCKS):
+            nc.vector.memset(windows[b][:, 0:8], 0.0)
+        for b in range(6, BLOCKS):
             nc.gpsimd.memset(windows[b][:], 0.0)
 
         w_loads = [(0, 128), (128, 384), (512, 512)]
@@ -130,6 +134,11 @@ def tile_list_hboth_none_kernel(tc, xT, w, wgt, wgo, offs, offs2, out):
         def store(b):
             nc.sync.dma_start(out[b * P : (b + 1) * P, :], windows[b][:])
 
+        def store_halves(b):
+            rows = slice(b * P, (b + 1) * P)
+            nc.sync.dma_start(out[rows, 0 : T // 2], windows[b][:, 0 : T // 2])
+            nc.scalar.dma_start(out[rows, T // 2 : T], windows[b][:, T // 2 : T])
+
         for i, h in ((0, 0), (0, 1), (1, 0), (1, 1), (2, 0), (2, 1), (3, 0)):
             gather(i, h)
         interleave(nc.vector.tensor_copy, x_grouped[0][:], gathered[0][:])
@@ -157,4 +166,4 @@ def tile_list_hboth_none_kernel(tc, xT, w, wgt, wgo, offs, offs2, out):
             scatter(b - 1, 1)
             store(b - 1)
         scatter(BLOCKS - 1, 1)
-        store(BLOCKS - 1)
+        store_halves(BLOCKS - 1)

import concourse.mybir as mybir

K, M, T, S = 512, 1024, 1024, 512
FLOPS = 2 * K * M * S

F32 = mybir.dt.float32
BF16 = mybir.dt.bfloat16
U32 = mybir.dt.uint32
U16 = mybir.dt.uint16
U8 = mybir.dt.uint8
FP8X4 = mybir.dt.float8_e4m3fn_x4
MULT = mybir.AluOpType.mult

P = 128
PACK = 4
HALF = S // 2
LIST_COLS = S // 16
HALF_COLS = LIST_COLS // 2
BLOCKS = M // P


def tile_list_hboth_none_kernel(tc, xT, w, wgt, wgo, offs, offs2, out):
    nc = tc.nc
    x_planes = xT.rearrange("(p i) t -> p i t", i=PACK)
    w_rows = w.rearrange("(p i) n -> p i n", i=PACK)

    with (
        tc.tile_pool(name="held", bufs=1) as held,
        tc.psum_pool(name="psum", bufs=1) as psum,
    ):
        list_in = held.tile([P, LIST_COLS], U16, name="list_in")
        list_out = held.tile([P, LIST_COLS], U16, name="list_out")
        wgt_half = [held.tile([P, HALF], F32, name=f"wgt{h}") for h in range(2)]
        wgo_all = held.tile([P, S], F32, name="wgo_all")
        planes = [held.tile([P, T], F32, name=f"plane{i}") for i in range(PACK)]
        windows = [held.tile([P, T], F32, name=f"window{b}") for b in range(BLOCKS)]

        nc.sync.dma_start(list_in[:], offs)
        nc.scalar.dma_start(wgt_half[0][:], wgt[:, 0:HALF])
        nc.sync.dma_start(planes[0][:], x_planes[:, 0, :])
        nc.scalar.dma_start(wgt_half[1][:], wgt[:, HALF:S])
        for i in range(1, PACK):
            nc.sync.dma_start(planes[i][:], x_planes[:, i, :])

        for b in range(6):
            nc.vector.memset(windows[b][:], 0.0)
        for b in range(6, BLOCKS):
            nc.vector.memset(windows[b][:, 0:8], 0.0)
        for b in range(6, BLOCKS):
            nc.gpsimd.memset(windows[b][:], 0.0)

        w_loads = [(0, 128), (128, 384), (512, 512)]
        w_raw = []
        for n, (c0, width) in enumerate(w_loads):
            raw = held.tile([P, PACK, width], F32, name=f"w_raw{n}")
            nc.sync.dma_start(raw[:], w_rows[:, :, c0 : c0 + width])
            w_raw.append(raw)
            if n == 0:
                nc.sync.dma_start(list_out[:], offs2)
                nc.sync.dma_start(wgo_all[:], wgo)

        gathered = [held.tile([P, PACK, HALF], F32, name=f"gathered{h}") for h in range(2)]
        x_grouped = [held.tile([P, HALF, PACK], BF16, align_bytes=64, name=f"x_grouped{h}") for h in range(2)]
        x_codes = held.tile([P, S], U32, align_bytes=64, name="x_codes")
        x_scales = held.tile([P, S], U8, align_bytes=64, name="x_scales")

        def gather(i, h):
            nc.vector.tensor_tensor(
                gathered[h][:, i, :],
                planes[i][:].indirect(list_in[:, h * HALF_COLS : (h + 1) * HALF_COLS]),
                wgt_half[h][:],
                MULT,
            )

        def interleave(copy, grouped, rows):
            copy(
                out=grouped.rearrange("p (c i) t -> p c t i", i=4),
                in_=rows.rearrange("p t (c i) -> p c t i", i=4),
            )

        def quantize_x(h):
            cols = slice(h * HALF, (h + 1) * HALF)
            nc.vector.quantize_mx(
                out=x_codes[:, cols].bitcast(FP8X4),
                scales=x_scales[:, cols],
                in_=x_grouped[h][:].rearrange("p c t -> p (c t)"),
            )

        w_codes = {}

        def prepare_w(n, c0, width):
            start = w_loads[n][0]
            grouped = held.tile([P, width, PACK], BF16, align_bytes=64, name=f"w_grouped{c0}")
            codes = held.tile([P, width], U32, align_bytes=64, name=f"w_codes{c0}")
            scales = held.tile([P, width], U8, align_bytes=64, name=f"w_scales{c0}")
            interleave(nc.scalar.copy, grouped[:], w_raw[n][:, :, c0 - start : c0 - start + width])
            nc.vector.quantize_mx(
                out=codes[:].bitcast(FP8X4),
                scales=scales[:],
                in_=grouped[:].rearrange("p c t -> p (c t)"),
            )
            for b in range(c0 // P, (c0 + width) // P):
                cols = slice(b * P - c0, (b + 1) * P - c0)
                w_codes[b] = (codes[:, cols].bitcast(FP8X4), scales[:, cols])

        y = {}

        def product(b, h0, h1):
            cols = slice(h0 * HALF, h1 * HALF)
            width = (h1 - h0) * HALF
            bank = psum.tile([P, width], F32, name=f"bank{b % 4}_{h0}" if b < 2 else f"wide{b % 4}")
            nc.tensor.matmul_mx(
                out=bank[:],
                lhsT=w_codes[b][0],
                lhsT_scale=w_codes[b][1],
                rhs=x_codes[:, cols].bitcast(FP8X4),
                rhs_scale=x_scales[:, cols],
                start=True,
                stop=True,
            )
            rows = held.tile([P, width], F32, name=f"y{b}_{h0}")
            nc.scalar.copy(out=rows[:], in_=bank[:])
            for h in range(h0, h1):
                y[b, h] = rows[:, (h - h0) * HALF : (h - h0 + 1) * HALF]

        def scatter(b, h):
            nc.vector.tensor_tensor(
                windows[b][:].indirect(list_out[:, h * HALF_COLS : (h + 1) * HALF_COLS]),
                y[b, h],
                wgo_all[:, h * HALF : (h + 1) * HALF],
                MULT,
            )

        def store(b):
            nc.sync.dma_start(out[b * P : (b + 1) * P, :], windows[b][:])

        def store_halves(b):
            rows = slice(b * P, (b + 1) * P)
            nc.sync.dma_start(out[rows, 0 : T // 2], windows[b][:, 0 : T // 2])
            nc.scalar.dma_start(out[rows, T // 2 : T], windows[b][:, T // 2 : T])

        for i, h in ((0, 0), (0, 1), (1, 0), (1, 1), (2, 0), (2, 1), (3, 0)):
            gather(i, h)
        interleave(nc.vector.tensor_copy, x_grouped[0][:], gathered[0][:])
        prepare_w(0, 0, 128)
        quantize_x(0)
        gather(3, 1)
        prepare_w(1, 128, 128)
        product(0, 0, 1)
        interleave(nc.scalar.copy, x_grouped[1][:], gathered[1][:])
        product(1, 0, 1)
        scatter(0, 0)
        quantize_x(1)
        scatter(1, 0)
        product(0, 1, 2)
        product(1, 1, 2)
        prepare_w(1, 256, 256)
        scatter(0, 1)
        store(0)
        product(2, 0, 2)
        prepare_w(2, 512, 512)
        for b in range(2, BLOCKS):
            if b + 1 < BLOCKS:
                product(b + 1, 0, 2)
            scatter(b, 0)
            scatter(b - 1, 1)
            store(b - 1)
        scatter(BLOCKS - 1, 1)
        store_halves(BLOCKS - 1)
